import numpy as np
import ml_dtypes


def mxq(x, axis, fmt="e4m3"):
    dtype, down = {"e4m3": (ml_dtypes.float8_e4m3fn, 7), "e5m2": (ml_dtypes.float8_e5m2, 14)}[fmt]
    v = np.moveaxis(np.asarray(x, np.float32).astype(ml_dtypes.bfloat16).astype(np.float64), axis, -1)
    blocks = v.reshape(v.shape[:-1] + (-1, 32))
    amax = np.abs(blocks).max(-1, keepdims=True)
    byte = np.maximum(np.where(amax > 0, np.frexp(amax)[1] - 1 + 127, 0) - down, 1)
    scale = np.exp2(byte - 127.0)
    codes = (blocks / scale).astype(np.float32).astype(dtype).astype(np.float64)
    return np.moveaxis((codes * scale).reshape(v.shape), -1, axis)


WIDE = False


def mx_kscale(k):
    if not WIDE:
        return np.ones(k)
    levels = np.array([10, -10, 5, -5, 0])
    if k % 512:
        return np.exp2(np.random.permutation(np.resize(levels, k // 32))).repeat(32)
    a = np.empty((k // 512, 16))
    for p in range(k // 512):
        a[p, :8] = np.random.permutation(np.resize(levels, 8))
        for g in range(8):
            far = levels[np.abs(levels - a[p, g]) >= 10]
            a[p, g + 8] = far[np.random.randint(len(far))]
    return np.exp2(a.ravel()).repeat(32)


def f64(x):
    return np.asarray(x).astype(np.float64)


def striped(idx):
    return np.tile(idx.reshape(-1, 16).T, (8, 1)).astype(np.uint16)


def unstriped(offs):
    return offs[:16].T.reshape(-1).astype(np.int64)


def striped8(idx):
    return np.concatenate([x.reshape(-1, 16).T for x in idx]).astype(np.uint16)


def runs(offs, k):
    lists = np.stack([offs[16 * r : 16 * r + 16].T.reshape(-1) for r in range(8)]).astype(np.int64)
    return lists[np.arange(k) % 512 // 64]


def pack_weight(w):
    k, n = w.shape
    w = f64(np.asarray(w, np.float32).astype(ml_dtypes.bfloat16)).reshape(k // 32, 32, n)
    amax = np.abs(w).max(1)
    byte = np.clip(np.where(amax > 0, np.frexp(amax)[1] - 1 + 127 - 7, 1), 1, 254)
    scaled = (w * np.exp2(127.0 - byte)[:, None, :]).reshape(k, n).astype(np.float32)
    words = np.ascontiguousarray(scaled.reshape(k // 512, 128, 4, n).transpose(0, 1, 3, 2)).astype(ml_dtypes.float8_e4m3fn).view(np.uint8)
    return words, np.ascontiguousarray(byte.astype(np.uint8).reshape(k // 512, 16, n))


def unpack_weight(words, scales):
    g, p, n, _ = words.shape
    vals = np.ascontiguousarray(words).view(ml_dtypes.float8_e4m3fn).astype(np.float64) * np.repeat(np.exp2(scales.astype(np.float64) - 127.0), 8, axis=1)[..., None]
    return vals.transpose(0, 1, 3, 2).reshape(g * 512, n)


E2M1 = np.array([0.0, 0.5, 1.0, 1.5, 2.0, 3.0, 4.0, 6.0, -0.0, -0.5, -1.0, -1.5, -2.0, -3.0, -4.0, -6.0])


def pack_fp4(w):
    k, n = w.shape
    w = f64(np.asarray(w, np.float32).astype(ml_dtypes.bfloat16)).reshape(k // 32, 32, n)
    amax = np.abs(w).max(1)
    mant, ex = np.frexp(amax / 6.0)
    byte = np.clip(np.where(amax > 0, np.where(mant > 0.5, ex, ex - 1) + 127, 1), 1, 254)
    scaled = (w * np.exp2(127.0 - byte)[:, None, :]).reshape(k, n).astype(np.float32)
    c = np.ascontiguousarray(scaled.reshape(k // 512, 128, 4, n).transpose(0, 1, 3, 2)).astype(ml_dtypes.float4_e2m1fn).view(np.uint8) & 0xF
    words = (c[..., 0::2] | (c[..., 1::2] << 4)).reshape(k // 512, 128, 2 * n)
    return np.ascontiguousarray(words), np.ascontiguousarray(byte.astype(np.uint8).reshape(k // 512, 16, n))


def unpack_fp4(words, scales):
    g, _, n = scales.shape
    words = np.ascontiguousarray(words).reshape(g, 128, n, 2)
    nib = np.empty((g, 128, n, 4), np.uint8)
    nib[..., 0::2] = words & 0xF
    nib[..., 1::2] = words >> 4
    vals = E2M1[nib] * np.repeat(np.exp2(scales.astype(np.float64) - 127.0), 8, axis=1)[..., None]
    return vals.transpose(0, 1, 3, 2).reshape(g * 512, n)


def planes(y):
    n, m = y.shape
    v = y.astype(np.float32).astype(ml_dtypes.bfloat16).astype(np.float64).reshape(n // 32, 32, m)
    top = np.abs(v).max(1)
    byte = np.clip(np.where(top > 0, np.frexp(top)[1] - 1 + 127 - 7, 1), 1, 254)
    codes = (v * np.exp2(127.0 - byte)[:, None, :]).reshape(n, m).astype(np.float32).astype(ml_dtypes.float8_e4m3fn).view(np.uint8)
    words = codes.reshape(n // 512, 128, 4, m).transpose(0, 1, 3, 2)
    return np.ascontiguousarray(words), np.ascontiguousarray(byte.astype(np.uint8).reshape(n // 512, 16, m))


K, T, S, N, H, W, J = 512, 2048, 512, 512, 512, 256, 512


def setup_inputs():
    n = np.random.standard_normal
    s = mx_kscale(K)[:, None]
    u = mx_kscale(S)
    packed_xT = pack_weight(n((K, T)) * s)
    packed_w1 = pack_fp4(n((S, N)) / np.sqrt(S) / u[:, None])
    perm = np.stack([np.random.permutation(H) for _ in range(8)])
    return {
        "x_words": packed_xT[0],
        "x_scales": packed_xT[1],
        "wa": (n((K, H)) / np.sqrt(K) / s).astype(np.float32),
        "gt": (np.random.uniform(0.5, 1.5, (S, 1)) * u[:, None]).astype(np.float32),
        "w1_words": packed_w1[0],
        "w1_scales": packed_w1[1],
        "tab": np.random.uniform(0.4, 1.4, (N, J)).astype(np.float32),
        "offs": striped(np.random.permutation(T)[:S]),
        "n1": striped8(perm[:, :W]),
        "n2": striped8(perm[:, W:]),
        "n3": striped8(np.random.randint(0, J, (8, H))),
        "n4": striped8(np.stack([np.random.permutation(H) for _ in range(8)])),
    }


def reference(x_words, x_scales, wa, gt, w1_words, w1_scales, tab, offs, n1, n2, n3, n4):
    xq = unpack_weight(x_words, x_scales)[:, unstriped(offs)]
    y = xq.T @ mxq(f64(wa), 0, "e4m3")
    pa = y[np.arange(S)[:, None], runs(n1, S)]
    pb = y[np.arange(S)[:, None], runs(n2, S)]
    ra = np.maximum(pa, pb)
    ds = y.copy()
    ds[np.arange(S)[:, None], runs(n1, S)] = ra
    z = f64(gt) * ds
    h = unpack_fp4(w1_words, w1_scales).T @ mxq(z, 0, "e4m3")
    out_0 = h * (f64(tab)[np.arange(N)[:, None], runs(n3, N)]) - (0.5 * (h[np.arange(N)[:, None], runs(n4, N)]))
    return (out_0,) + planes(out_0)

@@ -1,0 +1,214 @@
+from contextlib import ExitStack
+
+import concourse.mybir as mybir
+
+K, T, S, N, H, W, J = 512, 2048, 512, 512, 512, 256, 512
+FLOPS = 2 * K * S * H + 2 * S * N * H
+
+F32 = mybir.dt.float32
+BF16 = mybir.dt.bfloat16
+I32 = mybir.dt.int32
+U32 = mybir.dt.uint32
+U16 = mybir.dt.uint16
+U8 = mybir.dt.uint8
+FP8X4 = mybir.dt.float8_e4m3fn_x4
+FP4X4 = mybir.dt.float4_e2m1fn_x4
+ALU = mybir.AluOpType
+COPY = mybir.ActivationFunctionType.Copy
+
+P = 128
+PACK = 4
+HALF = 256
+
+
+def tile_picked_tokfillkindg_none_po_kernel(
+    tc, x_words, x_scales, wa, gt, w1_words, w1_scales, tab, offs, n1, n2, n3, n4, out_0, out_1, out_2
+):
+    nc = tc.nc
+    with ExitStack() as ctx:
+        sb = ctx.enter_context(tc.tile_pool(name="sb", bufs=1))
+        psum = ctx.enter_context(tc.psum_pool(name="psum", bufs=1))
+
+        offs_t = sb.tile([P, S // 16], U16, name="offs_t")
+        n1_t = sb.tile([P, W // 16], U16, name="n1_t")
+        n2_t = sb.tile([P, W // 16], U16, name="n2_t")
+        n3_t = sb.tile([P, H // 16], U16, name="n3_t")
+        n4_t = sb.tile([P, H // 16], U16, name="n4_t")
+
+        xw = sb.tile([P, T], U32, name="xw", align_bytes=64)
+        xs = sb.tile([P, T], U8, name="xs", align_bytes=64)
+        wa_raw = sb.tile([P, PACK, H], F32, name="wa_raw", align_bytes=64)
+        w1w_raw = sb.tile([P, 2 * N], U8, name="w1w_raw", align_bytes=64)
+        w1s_raw = sb.tile([P, N], U8, name="w1s_raw", align_bytes=64)
+        gt_t = sb.tile([P, PACK], F32, name="gt_t")
+        tab_t = [sb.tile([P, J], F32, name="tab%d" % t, align_bytes=64) for t in range(PACK)]
+
+        nc.vector.memset(xs[:].bitcast(I32), 0)
+        nc.vector.memset(w1s_raw[:].bitcast(I32), 0)
+
+        nc.sync.dma_start(offs_t[:], offs)
+        nc.sync.dma_start(wa_raw[:], wa.rearrange("(p j) c -> p j c", j=PACK))
+        for q in range(4):
+            nc.scalar.dma_start(xs[32 * q : 32 * q + 4, :].bitcast(I32), x_scales[0, 4 * q : 4 * q + 4, :].bitcast(I32))
+        nc.sync.dma_start(xw[:].bitcast(I32), x_words[0].rearrange("p n t -> p (n t)").bitcast(I32))
+        nc.scalar.dma_start(w1w_raw[:].bitcast(I32), w1_words[0].bitcast(I32))
+        for q in range(4):
+            nc.gpsimd.dma_start(w1s_raw[32 * q : 32 * q + 4, :].bitcast(I32), w1_scales[0, 4 * q : 4 * q + 4, :].bitcast(I32))
+        nc.sync.dma_start(n3_t[:], n3)
+        tab_v = tab.rearrange("(p t) c -> p t c", t=PACK)
+        nc.sync.dma_start(tab_t[0][:], tab_v[:, 0, :])
+        nc.sync.dma_start(n1_t[:], n1)
+        nc.sync.dma_start(n2_t[:], n2)
+        nc.sync.dma_start(gt_t[:], gt.rearrange("(p t) o -> p (t o)", t=PACK))
+        for t in range(1, PACK):
+            nc.sync.dma_start(tab_t[t][:], tab_v[:, t, :])
+        nc.sync.dma_start(n4_t[:], n4)
+
+        gs = sb.tile([P, S], U8, name="gs", align_bytes=64)
+        nc.vector.tensor_copy(gs[:].rearrange("p (t m) -> p m t", t=PACK), xs[:].indirect(offs_t[:]))
+
+        wa_b = sb.tile([P, H, PACK], BF16, name="wa_b", align_bytes=64)
+        wa_q = sb.tile([P, H], U32, name="wa_q", align_bytes=64)
+        wa_s = sb.tile([P, H], U8, name="wa_s", align_bytes=64)
+        SPLIT = 192
+        src = wa_raw[:].rearrange("p j (c i) -> p c j i", i=4)
+        dst = wa_b[:].rearrange("p (c i) j -> p c j i", i=4)
+        nc.scalar.copy(dst[:, : SPLIT // 4], src[:, : SPLIT // 4])
+        nc.vector.tensor_copy(dst[:, SPLIT // 4 :], src[:, SPLIT // 4 :])
+        nc.vector.quantize_mx(out=wa_q[:].bitcast(FP8X4), scales=wa_s[:], in_=wa_b[:].rearrange("p c j -> p (c j)"))
+
+        w1w = sb.tile([P, 2 * N], U8, name="w1w", align_bytes=64)
+        w1s = sb.tile([P, N], U8, name="w1s", align_bytes=64)
+        nc.scalar.copy(
+            w1w[:].bitcast(U16).rearrange("p (t m) -> p t m", t=PACK),
+            w1w_raw[:].bitcast(U16).rearrange("p (m t) -> p t m", t=PACK),
+        )
+        nc.vector.tensor_copy(w1s[:].rearrange("p (t m) -> p t m", t=PACK), w1s_raw[:].rearrange("p (m t) -> p t m", t=PACK))
+
+        gw = sb.tile([P, S], U32, name="gw", align_bytes=64)
+        nc.vector.tensor_copy(gw[:].rearrange("p (t m) -> p m t", t=PACK), xw[:].indirect(offs_t[:]))
+
+        y_ps = [psum.tile([P, H], F32, name="y_ps%d" % t) for t in range(PACK)]
+        for t in range(PACK):
+            cols = slice(t * P, (t + 1) * P)
+            nc.tensor.matmul_mx(
+                out=y_ps[t][:], lhsT=gw[:, cols].bitcast(FP8X4), lhsT_scale=gs[:, cols],
+                rhs=wa_q[:].bitcast(FP8X4), rhs_scale=wa_s[:], start=True, stop=True,
+            )
+
+        tabg = sb.tile([P, PACK, H], F32, name="tabg", align_bytes=64)
+
+        def tab_gather(t):
+            for u in range(2):
+                nc.scalar.activation(
+                    tabg[:, t, u * HALF : (u + 1) * HALF], tab_t[t][:].indirect(n3_t[:, 16 * u : 16 * u + 16]), COPY
+                )
+
+        tab_gather(0)
+
+        ds = [sb.tile([P, H], F32, name="ds%d" % t, align_bytes=64) for t in range(PACK)]
+        pa = [sb.tile([P, W], F32, name="pa%d" % t, align_bytes=64) for t in range(PACK)]
+        pb = [sb.tile([P, W], F32, name="pb%d" % t, align_bytes=64) for t in range(PACK)]
+        ra = [sb.tile([P, W], F32, name="ra%d" % t, align_bytes=64) for t in range(PACK)]
+        for t in range(PACK):
+            nc.scalar.copy(ds[t][:], y_ps[t][:])
+            nc.scalar.activation(pa[t][:], ds[t][:].indirect(n1_t[:]), COPY)
+            if t == 0:
+                nc.vector.tensor_copy(pb[t][:], ds[t][:].indirect(n2_t[:]))
+            else:
+                nc.scalar.activation(pb[t][:], ds[t][:].indirect(n2_t[:]), COPY)
+            nc.vector.tensor_tensor(ra[t][:], pa[t][:], pb[t][:], ALU.max)
+            nc.vector.tensor_copy(ds[t][:].indirect(n1_t[:]), ra[t][:])
+
+        zw = sb.tile([P, 2, H], F32, name="zw", align_bytes=64)
+
+        def z_round(t, cols):
+            out = zw[:, t // 2, cols].bitcast(BF16).rearrange("p (c e) -> p c e", e=2)[:, :, t % 2]
+            nc.scalar.activation(out, ds[t][:, cols], COPY, scale=gt_t[:, t : t + 1])
+
+        full = slice(0, H)
+        z_round(0, full)
+        z_round(1, full)
+        tab_gather(1)
+        z_round(2, full)
+        tab_gather(2)
+        z_b = sb.tile([P, H, 2], F32, name="z_b", align_bytes=64)
+        z_q = sb.tile([P, H], U32, name="z_q", align_bytes=64)
+        z_s = sb.tile([P, H], U8, name="z_s", align_bytes=64)
+        halves = [slice(0, HALF), slice(HALF, H)]
+        for c in halves:
+            z_round(3, c)
+        for c in halves:
+            nc.vector.tensor_copy(z_b[:, c, :], zw[:, :, c].rearrange("p u c -> p c u"))
+        for c in halves:
+            nc.vector.quantize_mx(
+                out=z_q[:, c].bitcast(FP8X4), scales=z_s[:, c],
+                in_=z_b[:, c, :].rearrange("p c u -> p (c u)").bitcast(BF16),
+            )
+        tab_gather(3)
+
+        h_ps = [psum.tile([P, H], F32, name="h_ps%d" % t) for t in range(PACK)]
+        for t in range(PACK):
+            nc.tensor.matmul_mx(
+                out=h_ps[t][:], lhsT=w1w[:, 2 * P * t : 2 * P * (t + 1)].bitcast(FP4X4), lhsT_scale=w1s[:, P * t : P * (t + 1)],
+                rhs=z_q[:].bitcast(FP8X4), rhs_scale=z_s[:], start=True, stop=True,
+            )
+
+        hs = [sb.tile([P, H], F32, name="hs%d" % t, align_bytes=64) for t in range(PACK)]
+        hm = sb.tile([P, PACK, H], F32, name="hm", align_bytes=64)
+        hg = sb.tile([P, PACK, H], F32, name="hg", align_bytes=64)
+        res = sb.tile([P, PACK, H], F32, name="res", align_bytes=64)
+
+        def h_copy(t):
+            nc.scalar.activation(hs[t][:], h_ps[t][:], COPY, scale=-0.5)
+
+        def h_mult(t):
+            nc.vector.tensor_tensor(hm[:, t, :], h_ps[t][:], tabg[:, t, :], ALU.mult)
+
+        def h_gather(t, u):
+            nc.scalar.activation(hg[:, t, halves[u]], hs[t][:].indirect(n4_t[:, 16 * u : 16 * u + 16]), COPY)
+
+        def h_add(t, u):
+            nc.vector.tensor_tensor(res[:, t, halves[u]], hm[:, t, halves[u]], hg[:, t, halves[u]], ALU.add)
+
+        o_b = sb.tile([P, H, PACK], BF16, name="o_b", align_bytes=64)
+        o_q = sb.tile([P, H], U32, name="o_q", align_bytes=64)
+        o_s = sb.tile([P, H], U8, name="o_s", align_bytes=64)
+        out_v = out_0.rearrange("(p t) c -> p t c", t=PACK)
+        words_v = out_1[0].rearrange("p n t -> p (n t)").bitcast(I32)
+
+        def finish(u):
+            c = halves[u]
+            nc.sync.dma_start(out_v[:, :, c], res[:, :, c])
+            nc.vector.tensor_copy(
+                o_b[:, c, :].rearrange("p (c i) j -> p c j i", i=4), res[:, :, c].rearrange("p j (c i) -> p c j i", i=4)
+            )
+            nc.vector.quantize_mx(
+                out=o_q[:, c].bitcast(FP8X4), scales=o_s[:, c], in_=o_b[:, c, :].rearrange("p c j -> p (c j)")
+            )
+            nc.sync.dma_start(words_v[:, c], o_q[:, c].bitcast(I32))
+
+        h_copy(0)
+        h_mult(1)
+        h_mult(0)
+        h_gather(0, 0)
+        h_copy(1)
+        h_mult(2)
+        h_gather(1, 0)
+        h_mult(3)
+        h_copy(2)
+        h_add(0, 0)
+        h_add(1, 0)
+        h_gather(2, 0)
+        h_copy(3)
+        h_add(2, 0)
+        h_gather(3, 0)
+        h_add(3, 0)
+        finish(0)
+        for t in range(PACK):
+            h_gather(t, 1)
+            h_add(t, 1)
+        finish(1)
+        for q in range(4):
+            eng = nc.sync if q % 2 == 0 else nc.scalar
+            eng.dma_start(out_2[0, 4 * q : 4 * q + 4, :].bitcast(I32), o_s[32 * q : 32 * q + 4, :].bitcast(I32))

@@ -27,6 +27,7 @@ def tile_picked_tokfillkindg_none_po_kernel(
     nc = tc.nc
     with ExitStack() as ctx:
         sb = ctx.enter_context(tc.tile_pool(name="sb", bufs=1))
+        reuse = ctx.enter_context(tc.tile_pool(name="reuse", bufs=1))
         psum = ctx.enter_context(tc.psum_pool(name="psum", bufs=1))
 
         offs_t = sb.tile([P, S // 16], U16, name="offs_t")
@@ -37,139 +38,180 @@ def tile_picked_tokfillkindg_none_po_kernel(
 
         xw = sb.tile([P, T], U32, name="xw", align_bytes=64)
         xs = sb.tile([P, T], U8, name="xs", align_bytes=64)
-        wa_raw = sb.tile([P, PACK, H], F32, name="wa_raw", align_bytes=64)
+        wa_raw = [
+            sb.tile([P, PACK, HALF], F32, name="wa_raw0", align_bytes=64),
+            reuse.tile([P, PACK, HALF], F32, name="wa_raw1", offset=0, align_bytes=64),
+        ]
+        halves = [slice(0, HALF), slice(HALF, H)]
         w1w_raw = sb.tile([P, 2 * N], U8, name="w1w_raw", align_bytes=64)
         w1s_raw = sb.tile([P, N], U8, name="w1s_raw", align_bytes=64)
         gt_t = sb.tile([P, PACK], F32, name="gt_t")
         tab_t = [sb.tile([P, J], F32, name="tab%d" % t, align_bytes=64) for t in range(PACK)]
 
-        nc.vector.memset(xs[:].bitcast(I32), 0)
-        nc.vector.memset(w1s_raw[:].bitcast(I32), 0)
+        nc.gpsimd.memset(xs[:].bitcast(I32), 0)
+        nc.gpsimd.memset(w1s_raw[:].bitcast(I32), 0)
 
-        nc.sync.dma_start(offs_t[:], offs)
-        nc.sync.dma_start(wa_raw[:], wa.rearrange("(p j) c -> p j c", j=PACK))
-        for q in range(4):
-            nc.scalar.dma_start(xs[32 * q : 32 * q + 4, :].bitcast(I32), x_scales[0, 4 * q : 4 * q + 4, :].bitcast(I32))
-        nc.sync.dma_start(xw[:].bitcast(I32), x_words[0].rearrange("p n t -> p (n t)").bitcast(I32))
-        nc.scalar.dma_start(w1w_raw[:].bitcast(I32), w1_words[0].bitcast(I32))
-        for q in range(4):
-            nc.gpsimd.dma_start(w1s_raw[32 * q : 32 * q + 4, :].bitcast(I32), w1_scales[0, 4 * q : 4 * q + 4, :].bitcast(I32))
-        nc.sync.dma_start(n3_t[:], n3)
         tab_v = tab.rearrange("(p t) c -> p t c", t=PACK)
+        wa_v = wa.rearrange("(p j) c -> p j c", j=PACK)
+        nc.sync.dma_start(xw[:].bitcast(I32), x_words[0].rearrange("p n t -> p (n t)").bitcast(I32))
+        for q in range(4):
+            nc.sync.dma_start(xs[32 * q : 32 * q + 4, :].bitcast(I32), x_scales[0, 4 * q : 4 * q + 4, :].bitcast(I32))
+        nc.sync.dma_start(offs_t[:], offs)
+        for u in range(2):
+            nc.sync.dma_start(wa_raw[u][:], wa_v[:, :, halves[u]])
+        nc.sync.dma_start(w1w_raw[:].bitcast(I32), w1_words[0].bitcast(I32))
+        nc.sync.dma_start(n3_t[:], n3)
         nc.sync.dma_start(tab_t[0][:], tab_v[:, 0, :])
         nc.sync.dma_start(n1_t[:], n1)
         nc.sync.dma_start(n2_t[:], n2)
-        nc.sync.dma_start(gt_t[:], gt.rearrange("(p t) o -> p (t o)", t=PACK))
         for t in range(1, PACK):
             nc.sync.dma_start(tab_t[t][:], tab_v[:, t, :])
+        nc.sync.dma_start(gt_t[:], gt.rearrange("(p t) o -> p (t o)", t=PACK))
         nc.sync.dma_start(n4_t[:], n4)
+        for q in range(4):
+            nc.sync.dma_start(w1s_raw[32 * q : 32 * q + 4, :].bitcast(I32), w1_scales[0, 4 * q : 4 * q + 4, :].bitcast(I32))
 
         gs = sb.tile([P, S], U8, name="gs", align_bytes=64)
         nc.vector.tensor_copy(gs[:].rearrange("p (t m) -> p m t", t=PACK), xs[:].indirect(offs_t[:]))
 
-        wa_b = sb.tile([P, H, PACK], BF16, name="wa_b", align_bytes=64)
+        gw = sb.tile([P, S], U32, name="gw", align_bytes=64)
+        nc.vector.tensor_copy(gw[:].rearrange("p (t m) -> p m t", t=PACK), xw[:].indirect(offs_t[:]))
+
+        wa_b = sb.tile([P, H * PACK], BF16, name="wa_b", align_bytes=64)
         wa_q = sb.tile([P, H], U32, name="wa_q", align_bytes=64)
         wa_s = sb.tile([P, H], U8, name="wa_s", align_bytes=64)
-        SPLIT = 192
-        src = wa_raw[:].rearrange("p j (c i) -> p c j i", i=4)
-        dst = wa_b[:].rearrange("p (c i) j -> p c j i", i=4)
-        nc.scalar.copy(dst[:, : SPLIT // 4], src[:, : SPLIT // 4])
-        nc.vector.tensor_copy(dst[:, SPLIT // 4 :], src[:, SPLIT // 4 :])
-        nc.vector.quantize_mx(out=wa_q[:].bitcast(FP8X4), scales=wa_s[:], in_=wa_b[:].rearrange("p c j -> p (c j)"))
+        SPLIT = 96
+        y_ps = [psum.tile([P, H], F32, name="y_ps%d" % t) for t in range(PACK)]
+        y0_first = psum.tile([P, HALF], F32, name="y0_first", tag="h_ps3")
+        for u, c in enumerate(halves):
+            grouped = wa_b[:, PACK * c.start : PACK * c.stop]
+            src = wa_raw[u][:].rearrange("p j (c i) -> p c j i", i=4)
+            dst = grouped.rearrange("p (c i j) -> p c j i", i=4, j=PACK)
+            if u == 0:
+                nc.scalar.copy(dst, src)
+            else:
+                nc.scalar.copy(dst[:, : SPLIT // 4], src[:, : SPLIT // 4])
+                nc.vector.tensor_copy(dst[:, SPLIT // 4 :], src[:, SPLIT // 4 :])
+        for u, c in enumerate(halves):
+            nc.vector.quantize_mx(out=wa_q[:, c].bitcast(FP8X4), scales=wa_s[:, c], in_=wa_b[:, PACK * c.start : PACK * c.stop])
 
-        w1w = sb.tile([P, 2 * N], U8, name="w1w", align_bytes=64)
-        w1s = sb.tile([P, N], U8, name="w1s", align_bytes=64)
+        def project(out, t, c):
+            cols = slice(t * P, (t + 1) * P)
+            nc.tensor.matmul_mx(
+                out=out, lhsT=gw[:, cols].bitcast(FP8X4), lhsT_scale=gs[:, cols],
+                rhs=wa_q[:, c].bitcast(FP8X4), rhs_scale=wa_s[:, c], start=True, stop=True,
+            )
+
+        project(y0_first[:], 0, halves[0])
+        project(y_ps[0][:, halves[1]], 0, halves[1])
+        for t in range(1, PACK):
+            project(y_ps[t][:], t, slice(0, H))
+
+        w1w = reuse.tile([P, 2 * N], U8, name="w1w", offset=0, align_bytes=64)
         nc.scalar.copy(
             w1w[:].bitcast(U16).rearrange("p (t m) -> p t m", t=PACK),
             w1w_raw[:].bitcast(U16).rearrange("p (m t) -> p t m", t=PACK),
         )
-        nc.vector.tensor_copy(w1s[:].rearrange("p (t m) -> p t m", t=PACK), w1s_raw[:].rearrange("p (m t) -> p t m", t=PACK))
 
-        gw = sb.tile([P, S], U32, name="gw", align_bytes=64)
-        nc.vector.tensor_copy(gw[:].rearrange("p (t m) -> p m t", t=PACK), xw[:].indirect(offs_t[:]))
+        tabg = [reuse.tile([P, H], F32, name="tabg0", offset=2048, align_bytes=64)]
+        tabg.extend(sb.tile([P, H], F32, name="tabg%d" % t, align_bytes=64) for t in range(1, PACK))
+        zw_all = sb.tile([P, 2 * H], F32, name="zw_all", align_bytes=64)
+        zw = [zw_all[:, :H], zw_all[:, H:]]
+        middle = slice(HALF // 2, HALF // 2 + W)
 
-        y_ps = [psum.tile([P, H], F32, name="y_ps%d" % t) for t in range(PACK)]
-        for t in range(PACK):
-            cols = slice(t * P, (t + 1) * P)
-            nc.tensor.matmul_mx(
-                out=y_ps[t][:], lhsT=gw[:, cols].bitcast(FP8X4), lhsT_scale=gs[:, cols],
-                rhs=wa_q[:].bitcast(FP8X4), rhs_scale=wa_s[:], start=True, stop=True,
-            )
+        def tab_gather(t, u):
+            nc.scalar.activation(tabg[t][:, halves[u]], tab_t[t][:].indirect(n3_t[:, 16 * u : 16 * u + 16]), COPY)
 
-        tabg = sb.tile([P, PACK, H], F32, name="tabg", align_bytes=64)
-
-        def tab_gather(t):
-            for u in range(2):
-                nc.scalar.activation(
-                    tabg[:, t, u * HALF : (u + 1) * HALF], tab_t[t][:].indirect(n3_t[:, 16 * u : 16 * u + 16]), COPY
-                )
-
-        tab_gather(0)
+        tab_gather(0, 0)
 
         ds = [sb.tile([P, H], F32, name="ds%d" % t, align_bytes=64) for t in range(PACK)]
-        pa = [sb.tile([P, W], F32, name="pa%d" % t, align_bytes=64) for t in range(PACK)]
-        pb = [sb.tile([P, W], F32, name="pb%d" % t, align_bytes=64) for t in range(PACK)]
+        pa2 = sb.tile([P, W], F32, name="pa2", tag="pa2", align_bytes=64)
+        pb2 = sb.tile([P, W], F32, name="pb2", align_bytes=64)
+        pa = [tabg[1][:, middle], tabg[3][:, middle], pa2[:], zw[1][:, halves[0]]]
+        pb = [tabg[2][:, middle], tabg[0][:, halves[1]], pb2[:], zw[1][:, halves[1]]]
         ra = [sb.tile([P, W], F32, name="ra%d" % t, align_bytes=64) for t in range(PACK)]
-        for t in range(PACK):
-            nc.scalar.copy(ds[t][:], y_ps[t][:])
-            nc.scalar.activation(pa[t][:], ds[t][:].indirect(n1_t[:]), COPY)
-            if t == 0:
-                nc.vector.tensor_copy(pb[t][:], ds[t][:].indirect(n2_t[:]))
-            else:
-                nc.scalar.activation(pb[t][:], ds[t][:].indirect(n2_t[:]), COPY)
-            nc.vector.tensor_tensor(ra[t][:], pa[t][:], pb[t][:], ALU.max)
-            nc.vector.tensor_copy(ds[t][:].indirect(n1_t[:]), ra[t][:])
 
-        zw = sb.tile([P, 2, H], F32, name="zw", align_bytes=64)
+        def z_out(t, cols):
+            return zw[t // 2][:, cols].bitcast(BF16).rearrange("p (c e) -> p c e", e=2)[:, :, t % 2]
 
-        def z_round(t, cols):
-            out = zw[:, t // 2, cols].bitcast(BF16).rearrange("p (c e) -> p c e", e=2)[:, :, t % 2]
-            nc.scalar.activation(out, ds[t][:, cols], COPY, scale=gt_t[:, t : t + 1])
+        def z_scalar(t, cols):
+            nc.scalar.activation(z_out(t, cols), ds[t][:, cols], COPY, scale=gt_t[:, t : t + 1])
+
+        def z_vector(t, cols):
+            nc.vector.tensor_scalar(z_out(t, cols), ds[t][:, cols], gt_t[:, t : t + 1], None, ALU.mult)
 
         full = slice(0, H)
-        z_round(0, full)
-        z_round(1, full)
-        tab_gather(1)
-        z_round(2, full)
-        tab_gather(2)
+        nc.scalar.copy(ds[0][:, halves[0]], y0_first[:])
+        nc.vector.tensor_copy(ds[0][:, halves[1]], y_ps[0][:, halves[1]])
+        for t in range(PACK):
+            if t == 1:
+                nc.scalar.copy(ds[1][:], y_ps[1][:])
+            if t in (1, 2):
+                nc.scalar.copy(ds[t + 1][:], y_ps[t + 1][:])
+            nc.scalar.activation(pa[t], ds[t][:].indirect(n1_t[:]), COPY)
+            if t == 0:
+                nc.vector.tensor_copy(pb[t], ds[t][:].indirect(n2_t[:]))
+            else:
+                nc.scalar.activation(pb[t], ds[t][:].indirect(n2_t[:]), COPY)
+            nc.vector.tensor_tensor(ra[t][:], pa[t], pb[t], ALU.max)
+            if t == 2:
+                w1s = sb.tile([P, N], U8, name="w1s", tag="pa2", align_bytes=64)
+                nc.vector.tensor_copy(
+                    w1s[:].rearrange("p (t m) -> p t m", t=PACK), w1s_raw[:].rearrange("p (m t) -> p t m", t=PACK)
+                )
+            if t == 3:
+                z_vector(2, full)
+            nc.vector.tensor_copy(ds[t][:].indirect(n1_t[:]), ra[t][:])
+
+        z_scalar(0, full)
+        z_scalar(1, full)
+
+        tab_gather(0, 1)
+        for t in range(1, PACK):
+            tab_gather(t, 0)
+            tab_gather(t, 1)
+
         z_b = sb.tile([P, H, 2], F32, name="z_b", align_bytes=64)
         z_q = sb.tile([P, H], U32, name="z_q", align_bytes=64)
         z_s = sb.tile([P, H], U8, name="z_s", align_bytes=64)
-        halves = [slice(0, HALF), slice(HALF, H)]
         for c in halves:
-            z_round(3, c)
+            z_vector(3, c)
         for c in halves:
-            nc.vector.tensor_copy(z_b[:, c, :], zw[:, :, c].rearrange("p u c -> p c u"))
+            nc.vector.tensor_copy(z_b[:, c, :], zw_all[:].rearrange("p (u c) -> p c u", u=2)[:, c, :])
         for c in halves:
             nc.vector.quantize_mx(
                 out=z_q[:, c].bitcast(FP8X4), scales=z_s[:, c],
                 in_=z_b[:, c, :].rearrange("p c u -> p (c u)").bitcast(BF16),
             )
-        tab_gather(3)
 
-        h_ps = [psum.tile([P, H], F32, name="h_ps%d" % t) for t in range(PACK)]
-        for t in range(PACK):
-            nc.tensor.matmul_mx(
-                out=h_ps[t][:], lhsT=w1w[:, 2 * P * t : 2 * P * (t + 1)].bitcast(FP4X4), lhsT_scale=w1s[:, P * t : P * (t + 1)],
-                rhs=z_q[:].bitcast(FP8X4), rhs_scale=z_s[:], start=True, stop=True,
-            )
+        h_ps = [psum.tile([P, H], F32, name="h_ps%d" % t, tag="h_ps%d" % t) for t in range(PACK)]
+        for pair in range(2):
+            for c in halves:
+                for t in (2 * pair, 2 * pair + 1):
+                    nc.tensor.matmul_mx(
+                        out=h_ps[t][:, c], lhsT=w1w[:, 2 * P * t : 2 * P * (t + 1)].bitcast(FP4X4),
+                        lhsT_scale=w1s[:, P * t : P * (t + 1)],
+                        rhs=z_q[:, c].bitcast(FP8X4), rhs_scale=z_s[:, c], start=True, stop=True,
+                    )
 
         hs = [sb.tile([P, H], F32, name="hs%d" % t, align_bytes=64) for t in range(PACK)]
         hm = sb.tile([P, PACK, H], F32, name="hm", align_bytes=64)
         hg = sb.tile([P, PACK, H], F32, name="hg", align_bytes=64)
         res = sb.tile([P, PACK, H], F32, name="res", align_bytes=64)
 
+        chunks = [slice(P * k, P * (k + 1)) for k in range(4)]
+
         def h_copy(t):
-            nc.scalar.activation(hs[t][:], h_ps[t][:], COPY, scale=-0.5)
+            if t % 2 == 0:
+                nc.scalar.activation(hs[t][:], h_ps[t][:], COPY, scale=-0.5)
+            else:
+                nc.vector.tensor_scalar(hs[t][:], h_ps[t][:], -0.5, None, ALU.mult)
 
         def h_mult(t):
-            nc.vector.tensor_tensor(hm[:, t, :], h_ps[t][:], tabg[:, t, :], ALU.mult)
+            nc.vector.tensor_tensor(hm[:, t, :], h_ps[t][:], tabg[t][:], ALU.mult)
 
-        def h_gather(t, u):
-            nc.scalar.activation(hg[:, t, halves[u]], hs[t][:].indirect(n4_t[:, 16 * u : 16 * u + 16]), COPY)
-
-        def h_add(t, u):
-            nc.vector.tensor_tensor(res[:, t, halves[u]], hm[:, t, halves[u]], hg[:, t, halves[u]], ALU.add)
+        def h_gather(t, c):
+            nc.scalar.activation(hg[:, t, c], hs[t][:].indirect(n4_t[:, c.start // 16 : c.stop // 16]), COPY)
 
         o_b = sb.tile([P, H, PACK], BF16, name="o_b", align_bytes=64)
         o_q = sb.tile([P, H], U32, name="o_q", align_bytes=64)
@@ -177,38 +219,40 @@ def tile_picked_tokfillkindg_none_po_kernel(
         out_v = out_0.rearrange("(p t) c -> p t c", t=PACK)
         words_v = out_1[0].rearrange("p n t -> p (n t)").bitcast(I32)
 
-        def finish(u):
-            c = halves[u]
-            nc.sync.dma_start(out_v[:, :, c], res[:, :, c])
+        def h_add(c):
+            nc.vector.tensor_tensor(res[:, :, c], hm[:, :, c], hg[:, :, c], ALU.add)
+
+        def o_round(c):
             nc.vector.tensor_copy(
                 o_b[:, c, :].rearrange("p (c i) j -> p c j i", i=4), res[:, :, c].rearrange("p j (c i) -> p c j i", i=4)
             )
+
+        def o_quantise(c):
             nc.vector.quantize_mx(
                 out=o_q[:, c].bitcast(FP8X4), scales=o_s[:, c], in_=o_b[:, c, :].rearrange("p c j -> p (c j)")
             )
-            nc.sync.dma_start(words_v[:, c], o_q[:, c].bitcast(I32))
 
         h_copy(0)
-        h_mult(1)
-        h_mult(0)
-        h_gather(0, 0)
         h_copy(1)
-        h_mult(2)
-        h_gather(1, 0)
-        h_mult(3)
         h_copy(2)
-        h_add(0, 0)
-        h_add(1, 0)
-        h_gather(2, 0)
+        h_mult(0)
         h_copy(3)
-        h_add(2, 0)
-        h_gather(3, 0)
-        h_add(3, 0)
-        finish(0)
-        for t in range(PACK):
-            h_gather(t, 1)
-            h_add(t, 1)
-        finish(1)
+        for t in range(1, PACK):
+            h_mult(t)
+        for step in range(6):
+            if step < 4:
+                for t in range(PACK):
+                    h_gather(t, chunks[step])
+                h_add(chunks[step])
+                if step % 2 == 1:
+                    nc.sync.dma_start(out_v[:, :, halves[step // 2]], res[:, :, halves[step // 2]])
+            if 1 <= step < 5:
+                o_round(chunks[step - 1])
+            if step >= 2:
+                o_quantise(chunks[step - 2])
+                if step % 2 == 1:
+                    c = halves[(step - 2) // 2]
+                    nc.sync.dma_start(words_v[:, c], o_q[:, c].bitcast(I32))
         for q in range(4):
             eng = nc.sync if q % 2 == 0 else nc.scalar
             eng.dma_start(out_2[0, 4 * q : 4 * q + 4, :].bitcast(I32), o_s[32 * q : 32 * q + 4, :].bitcast(I32))

@@ -80,8 +80,8 @@ def tile_picked_tokfillkindg_none_po_kernel(
         wa_b = sb.tile([P, H * PACK], BF16, name="wa_b", align_bytes=64)
         wa_q = sb.tile([P, H], U32, name="wa_q", align_bytes=64)
         wa_s = sb.tile([P, H], U8, name="wa_s", align_bytes=64)
-        SPLIT = 96
-        y_ps = [psum.tile([P, H], F32, name="y_ps%d" % t) for t in range(PACK)]
+        SPLIT = 144
+        y_ps = [psum.tile([P, H], F32, name="y_ps%d" % t, tag="y_ps%d" % t) for t in range(PACK)]
         y0_first = psum.tile([P, HALF], F32, name="y0_first", tag="h_ps3")
         for u, c in enumerate(halves):
             grouped = wa_b[:, PACK * c.start : PACK * c.stop]
@@ -184,12 +184,15 @@ def tile_picked_tokfillkindg_none_po_kernel(
                 in_=z_b[:, c, :].rearrange("p c u -> p (c u)").bitcast(BF16),
             )
 
-        h_ps = [psum.tile([P, H], F32, name="h_ps%d" % t, tag="h_ps%d" % t) for t in range(PACK)]
+        h_ps = [
+            [psum.tile([P, HALF], F32, name="h_ps%d_%d" % (t, u), tag=("y_ps%d", "h_ps%d")[u] % t) for u in range(2)]
+            for t in range(PACK)
+        ]
         for pair in range(2):
-            for c in halves:
+            for u, c in enumerate(halves):
                 for t in (2 * pair, 2 * pair + 1):
                     nc.tensor.matmul_mx(
-                        out=h_ps[t][:, c], lhsT=w1w[:, 2 * P * t : 2 * P * (t + 1)].bitcast(FP4X4),
+                        out=h_ps[t][u][:], lhsT=w1w[:, 2 * P * t : 2 * P * (t + 1)].bitcast(FP4X4),
                         lhsT_scale=w1s[:, P * t : P * (t + 1)],
                         rhs=z_q[:, c].bitcast(FP8X4), rhs_scale=z_s[:, c], start=True, stop=True,
                     )
@@ -201,14 +204,14 @@ def tile_picked_tokfillkindg_none_po_kernel(
 
         chunks = [slice(P * k, P * (k + 1)) for k in range(4)]
 
-        def h_copy(t):
+        def h_copy(t, u):
             if t % 2 == 0:
-                nc.scalar.activation(hs[t][:], h_ps[t][:], COPY, scale=-0.5)
+                nc.scalar.activation(hs[t][:, halves[u]], h_ps[t][u][:], COPY, scale=-0.5)
             else:
-                nc.vector.tensor_scalar(hs[t][:], h_ps[t][:], -0.5, None, ALU.mult)
+                nc.vector.tensor_scalar(hs[t][:, halves[u]], h_ps[t][u][:], -0.5, None, ALU.mult)
 
-        def h_mult(t):
-            nc.vector.tensor_tensor(hm[:, t, :], h_ps[t][:], tabg[t][:], ALU.mult)
+        def h_mult(t, u):
+            nc.vector.tensor_tensor(hm[:, t, halves[u]], h_ps[t][u][:], tabg[t][:, halves[u]], ALU.mult)
 
         def h_gather(t, c):
             nc.scalar.activation(hg[:, t, c], hs[t][:].indirect(n4_t[:, c.start // 16 : c.stop // 16]), COPY)
@@ -222,37 +225,38 @@ def tile_picked_tokfillkindg_none_po_kernel(
         def h_add(c):
             nc.vector.tensor_tensor(res[:, :, c], hm[:, :, c], hg[:, :, c], ALU.add)
 
-        def o_round(c):
-            nc.vector.tensor_copy(
-                o_b[:, c, :].rearrange("p (c i) j -> p c j i", i=4), res[:, :, c].rearrange("p j (c i) -> p c j i", i=4)
-            )
+        def o_round(c, copy):
+            copy(o_b[:, c, :].rearrange("p (c i) j -> p c j i", i=4), res[:, :, c].rearrange("p j (c i) -> p c j i", i=4))
 
         def o_quantise(c):
             nc.vector.quantize_mx(
                 out=o_q[:, c].bitcast(FP8X4), scales=o_s[:, c], in_=o_b[:, c, :].rearrange("p c j -> p (c j)")
             )
 
-        h_copy(0)
-        h_copy(1)
-        h_copy(2)
-        h_mult(0)
-        h_copy(3)
-        for t in range(1, PACK):
-            h_mult(t)
+        for pair in range(2):
+            for u in range(2):
+                for t in (2 * pair, 2 * pair + 1):
+                    h_copy(t, u)
+        for u in range(2):
+            for t in range(PACK):
+                h_mult(t, u)
         for step in range(6):
             if step < 4:
                 for t in range(PACK):
                     h_gather(t, chunks[step])
                 h_add(chunks[step])
-                if step % 2 == 1:
-                    nc.sync.dma_start(out_v[:, :, halves[step // 2]], res[:, :, halves[step // 2]])
+                if step >= 1:
+                    c = halves[0] if step == 1 else chunks[step]
+                    nc.sync.dma_start(out_v[:, :, c], res[:, :, c])
+            if step == 4:
+                o_quantise(chunks[1])
             if 1 <= step < 5:
-                o_round(chunks[step - 1])
-            if step >= 2:
+                o_round(chunks[step - 1], nc.scalar.copy if step == 3 else nc.vector.tensor_copy)
+            if step in (2, 4, 5):
                 o_quantise(chunks[step - 2])
-                if step % 2 == 1:
-                    c = halves[(step - 2) // 2]
-                    nc.sync.dma_start(words_v[:, c], o_q[:, c].bitcast(I32))
+            if step >= 4:
+                c = slice(0, 384) if step == 4 else chunks[3]
+                nc.sync.dma_start(words_v[:, c], o_q[:, c].bitcast(I32))
         for q in range(4):
-            eng = nc.sync if q % 2 == 0 else nc.scalar
+            eng = nc.scalar if q % 2 == 0 else nc.sync
             eng.dma_start(out_2[0, 4 * q : 4 * q + 4, :].bitcast(I32), o_s[32 * q : 32 * q + 4, :].bitcast(I32))

@@ -82,7 +82,7 @@ def tile_picked_tokfillkindg_none_po_kernel(
         wa_s = sb.tile([P, H], U8, name="wa_s", align_bytes=64)
         SPLIT = 144
         y_ps = [psum.tile([P, H], F32, name="y_ps%d" % t, tag="y_ps%d" % t) for t in range(PACK)]
-        y0_first = psum.tile([P, HALF], F32, name="y0_first", tag="h_ps3")
+        y_first = [psum.tile([P, HALF], F32, name="y_first%d" % t, tag="h_ps%d" % (2 + t)) for t in range(2)]
         for u, c in enumerate(halves):
             grouped = wa_b[:, PACK * c.start : PACK * c.stop]
             src = wa_raw[u][:].rearrange("p j (c i) -> p c j i", i=4)
@@ -102,9 +102,11 @@ def tile_picked_tokfillkindg_none_po_kernel(
                 rhs=wa_q[:, c].bitcast(FP8X4), rhs_scale=wa_s[:, c], start=True, stop=True,
             )
 
-        project(y0_first[:], 0, halves[0])
-        project(y_ps[0][:, halves[1]], 0, halves[1])
-        for t in range(1, PACK):
+        for t in range(2):
+            project(y_first[t][:], t, halves[0])
+        for t in range(2):
+            project(y_ps[t][:, halves[1]], t, halves[1])
+        for t in range(2, PACK):
             project(y_ps[t][:], t, slice(0, H))
 
         w1w = reuse.tile([P, 2 * N], U8, name="w1w", offset=0, align_bytes=64)
@@ -141,11 +143,11 @@ def tile_picked_tokfillkindg_none_po_kernel(
             nc.vector.tensor_scalar(z_out(t, cols), ds[t][:, cols], gt_t[:, t : t + 1], None, ALU.mult)
 
         full = slice(0, H)
-        nc.scalar.copy(ds[0][:, halves[0]], y0_first[:])
+        nc.scalar.copy(ds[0][:, halves[0]], y_first[0][:])
+        nc.vector.tensor_copy(ds[1][:, halves[0]], y_first[1][:])
         nc.vector.tensor_copy(ds[0][:, halves[1]], y_ps[0][:, halves[1]])
+        nc.scalar.copy(ds[1][:, halves[1]], y_ps[1][:, halves[1]])
         for t in range(PACK):
-            if t == 1:
-                nc.scalar.copy(ds[1][:], y_ps[1][:])
             if t in (1, 2):
                 nc.scalar.copy(ds[t + 1][:], y_ps[t + 1][:])
             nc.scalar.activation(pa[t], ds[t][:].indirect(n1_t[:]), COPY)
@@ -205,16 +207,22 @@ def tile_picked_tokfillkindg_none_po_kernel(
         chunks = [slice(P * k, P * (k + 1)) for k in range(4)]
 
         def h_copy(t, u):
-            if t % 2 == 0:
-                nc.scalar.activation(hs[t][:, halves[u]], h_ps[t][u][:], COPY, scale=-0.5)
-            else:
-                nc.vector.tensor_scalar(hs[t][:, halves[u]], h_ps[t][u][:], -0.5, None, ALU.mult)
+            copy = nc.scalar.copy if t == 0 else nc.vector.tensor_copy
+            copy(hs[t][:, halves[u]], h_ps[t][u][:])
 
         def h_mult(t, u):
-            nc.vector.tensor_tensor(hm[:, t, halves[u]], h_ps[t][u][:], tabg[t][:, halves[u]], ALU.mult)
+            c = halves[u]
+            if t < 2:
+                nc.gpsimd.tensor_tensor(hm[:, t, c], hs[t][:, c], tabg[t][:, c], ALU.mult)
+            else:
+                nc.vector.tensor_tensor(hm[:, t, c], h_ps[t][u][:], tabg[t][:, c], ALU.mult)
 
         def h_gather(t, c):
-            nc.scalar.activation(hg[:, t, c], hs[t][:].indirect(n4_t[:, c.start // 16 : c.stop // 16]), COPY)
+            picked = hs[t][:].indirect(n4_t[:, c.start // 16 : c.stop // 16])
+            if (t, c) == (2, chunks[0]):
+                nc.vector.tensor_copy(hg[:, t, c], picked)
+            else:
+                nc.scalar.activation(hg[:, t, c], picked, COPY)
 
         o_b = sb.tile([P, H, PACK], BF16, name="o_b", align_bytes=64)
         o_q = sb.tile([P, H], U32, name="o_q", align_bytes=64)
@@ -222,8 +230,8 @@ def tile_picked_tokfillkindg_none_po_kernel(
         out_v = out_0.rearrange("(p t) c -> p t c", t=PACK)
         words_v = out_1[0].rearrange("p n t -> p (n t)").bitcast(I32)
 
-        def h_add(c):
-            nc.vector.tensor_tensor(res[:, :, c], hm[:, :, c], hg[:, :, c], ALU.add)
+        def h_add(rows, c):
+            nc.vector.scalar_tensor_tensor(res[:, rows, c], hg[:, rows, c], -0.5, hm[:, rows, c], ALU.mult, ALU.add)
 
         def o_round(c, copy):
             copy(o_b[:, c, :].rearrange("p (c i) j -> p c j i", i=4), res[:, :, c].rearrange("p j (c i) -> p c j i", i=4))
@@ -240,14 +248,20 @@ def tile_picked_tokfillkindg_none_po_kernel(
         for u in range(2):
             for t in range(PACK):
                 h_mult(t, u)
+        early, late = slice(0, 2), slice(2, PACK)
+        for c in halves:
+            for t in range(2):
+                h_gather(t, c)
+            h_add(early, c)
+        nc.sync.dma_start(out_v[:, early, :], res[:, early, :])
         for step in range(6):
             if step < 4:
-                for t in range(PACK):
+                for t in range(2, PACK):
                     h_gather(t, chunks[step])
-                h_add(chunks[step])
-                if step >= 1:
-                    c = halves[0] if step == 1 else chunks[step]
-                    nc.sync.dma_start(out_v[:, :, c], res[:, :, c])
+                h_add(late, chunks[step])
+                if step >= 2:
+                    c = slice(0, 384) if step == 2 else chunks[step]
+                    nc.sync.dma_start(out_v[:, late, c], res[:, late, c])
             if step == 4:
                 o_quantise(chunks[1])
             if 1 <= step < 5:

from contextlib import ExitStack

import concourse.mybir as mybir

K, T, S, N, H, W, J = 512, 2048, 512, 512, 512, 256, 512
FLOPS = 2 * K * S * H + 2 * S * N * H

F32 = mybir.dt.float32
BF16 = mybir.dt.bfloat16
I32 = mybir.dt.int32
U32 = mybir.dt.uint32
U16 = mybir.dt.uint16
U8 = mybir.dt.uint8
FP8X4 = mybir.dt.float8_e4m3fn_x4
FP4X4 = mybir.dt.float4_e2m1fn_x4
ALU = mybir.AluOpType
COPY = mybir.ActivationFunctionType.Copy

P = 128
PACK = 4
HALF = 256


def tile_picked_tokfillkindg_none_po_kernel(
    tc, x_words, x_scales, wa, gt, w1_words, w1_scales, tab, offs, n1, n2, n3, n4, out_0, out_1, out_2
):
    nc = tc.nc
    with ExitStack() as ctx:
        sb = ctx.enter_context(tc.tile_pool(name="sb", bufs=1))
        reuse = ctx.enter_context(tc.tile_pool(name="reuse", bufs=1))
        psum = ctx.enter_context(tc.psum_pool(name="psum", bufs=1))

        offs_t = sb.tile([P, S // 16], U16, name="offs_t")
        n1_t = sb.tile([P, W // 16], U16, name="n1_t")
        n2_t = sb.tile([P, W // 16], U16, name="n2_t")
        n3_t = sb.tile([P, H // 16], U16, name="n3_t")
        n4_t = sb.tile([P, H // 16], U16, name="n4_t")

        xw = sb.tile([P, T], U32, name="xw", align_bytes=64)
        xs = sb.tile([P, T], U8, name="xs", align_bytes=64)
        wa_raw = [
            sb.tile([P, PACK, HALF], F32, name="wa_raw0", align_bytes=64),
            reuse.tile([P, PACK, HALF], F32, name="wa_raw1", offset=0, align_bytes=64),
        ]
        halves = [slice(0, HALF), slice(HALF, H)]
        w1w_raw = sb.tile([P, 2 * N], U8, name="w1w_raw", align_bytes=64)
        w1s_raw = sb.tile([P, N], U8, name="w1s_raw", align_bytes=64)
        gt_t = sb.tile([P, PACK], F32, name="gt_t")
        tab_t = [sb.tile([P, J], F32, name="tab%d" % t, align_bytes=64) for t in range(PACK)]

        nc.gpsimd.memset(xs[:].bitcast(I32), 0)
        nc.gpsimd.memset(w1s_raw[:].bitcast(I32), 0)

        tab_v = tab.rearrange("(p t) c -> p t c", t=PACK)
        wa_v = wa.rearrange("(p j) c -> p j c", j=PACK)
        nc.sync.dma_start(xw[:].bitcast(I32), x_words[0].rearrange("p n t -> p (n t)").bitcast(I32))
        for q in range(4):
            nc.sync.dma_start(xs[32 * q : 32 * q + 4, :].bitcast(I32), x_scales[0, 4 * q : 4 * q + 4, :].bitcast(I32))
        nc.sync.dma_start(offs_t[:], offs)
        for u in range(2):
            nc.sync.dma_start(wa_raw[u][:], wa_v[:, :, halves[u]])
        nc.sync.dma_start(w1w_raw[:].bitcast(I32), w1_words[0].bitcast(I32))
        nc.sync.dma_start(n3_t[:], n3)
        nc.sync.dma_start(tab_t[0][:], tab_v[:, 0, :])
        nc.sync.dma_start(n1_t[:], n1)
        nc.sync.dma_start(n2_t[:], n2)
        for t in range(1, PACK):
            nc.sync.dma_start(tab_t[t][:], tab_v[:, t, :])
        nc.sync.dma_start(gt_t[:], gt.rearrange("(p t) o -> p (t o)", t=PACK))
        nc.sync.dma_start(n4_t[:], n4)
        for q in range(4):
            nc.sync.dma_start(w1s_raw[32 * q : 32 * q + 4, :].bitcast(I32), w1_scales[0, 4 * q : 4 * q + 4, :].bitcast(I32))

        gs = sb.tile([P, S], U8, name="gs", align_bytes=64)
        nc.vector.tensor_copy(gs[:].rearrange("p (t m) -> p m t", t=PACK), xs[:].indirect(offs_t[:]))

        gw = sb.tile([P, S], U32, name="gw", align_bytes=64)
        nc.vector.tensor_copy(gw[:].rearrange("p (t m) -> p m t", t=PACK), xw[:].indirect(offs_t[:]))

        wa_b = sb.tile([P, H * PACK], BF16, name="wa_b", align_bytes=64)
        wa_q = sb.tile([P, H], U32, name="wa_q", align_bytes=64)
        wa_s = sb.tile([P, H], U8, name="wa_s", align_bytes=64)
        SPLIT = 144
        y_ps = [psum.tile([P, H], F32, name="y_ps%d" % t, tag="y_ps%d" % t) for t in range(PACK)]
        y_first = [psum.tile([P, HALF], F32, name="y_first%d" % t, tag="h_ps%d" % (2 + t)) for t in range(2)]
        for u, c in enumerate(halves):
            grouped = wa_b[:, PACK * c.start : PACK * c.stop]
            src = wa_raw[u][:].rearrange("p j (c i) -> p c j i", i=4)
            dst = grouped.rearrange("p (c i j) -> p c j i", i=4, j=PACK)
            if u == 0:
                nc.scalar.copy(dst, src)
            else:
                nc.scalar.copy(dst[:, : SPLIT // 4], src[:, : SPLIT // 4])
                nc.vector.tensor_copy(dst[:, SPLIT // 4 :], src[:, SPLIT // 4 :])
        for u, c in enumerate(halves):
            nc.vector.quantize_mx(out=wa_q[:, c].bitcast(FP8X4), scales=wa_s[:, c], in_=wa_b[:, PACK * c.start : PACK * c.stop])

        def project(out, t, c):
            cols = slice(t * P, (t + 1) * P)
            nc.tensor.matmul_mx(
                out=out, lhsT=gw[:, cols].bitcast(FP8X4), lhsT_scale=gs[:, cols],
                rhs=wa_q[:, c].bitcast(FP8X4), rhs_scale=wa_s[:, c], start=True, stop=True,
            )

        for t in range(2):
            project(y_first[t][:], t, halves[0])
        for t in range(2):
            project(y_ps[t][:, halves[1]], t, halves[1])
        for t in range(2, PACK):
            project(y_ps[t][:], t, slice(0, H))

        w1w = reuse.tile([P, 2 * N], U8, name="w1w", offset=0, align_bytes=64)
        nc.scalar.copy(
            w1w[:].bitcast(U16).rearrange("p (t m) -> p t m", t=PACK),
            w1w_raw[:].bitcast(U16).rearrange("p (m t) -> p t m", t=PACK),
        )

        tabg = [reuse.tile([P, H], F32, name="tabg0", offset=2048, align_bytes=64)]
        tabg.extend(sb.tile([P, H], F32, name="tabg%d" % t, align_bytes=64) for t in range(1, PACK))
        zw_all = sb.tile([P, 2 * H], F32, name="zw_all", align_bytes=64)
        zw = [zw_all[:, :H], zw_all[:, H:]]
        middle = slice(HALF // 2, HALF // 2 + W)

        def tab_gather(t, u):
            nc.scalar.activation(tabg[t][:, halves[u]], tab_t[t][:].indirect(n3_t[:, 16 * u : 16 * u + 16]), COPY)

        tab_gather(0, 0)

        ds = [sb.tile([P, H], F32, name="ds%d" % t, align_bytes=64) for t in range(PACK)]
        pa2 = sb.tile([P, W], F32, name="pa2", tag="pa2", align_bytes=64)
        pb2 = sb.tile([P, W], F32, name="pb2", align_bytes=64)
        pa = [tabg[1][:, middle], tabg[3][:, middle], pa2[:], zw[1][:, halves[0]]]
        pb = [tabg[2][:, middle], tabg[0][:, halves[1]], pb2[:], zw[1][:, halves[1]]]
        ra = [sb.tile([P, W], F32, name="ra%d" % t, align_bytes=64) for t in range(PACK)]

        def z_out(t, cols):
            return zw[t // 2][:, cols].bitcast(BF16).rearrange("p (c e) -> p c e", e=2)[:, :, t % 2]

        def z_scalar(t, cols):
            nc.scalar.activation(z_out(t, cols), ds[t][:, cols], COPY, scale=gt_t[:, t : t + 1])

        def z_vector(t, cols):
            nc.vector.tensor_scalar(z_out(t, cols), ds[t][:, cols], gt_t[:, t : t + 1], None, ALU.mult)

        full = slice(0, H)
        nc.scalar.copy(ds[0][:, halves[0]], y_first[0][:])
        nc.vector.tensor_copy(ds[1][:, halves[0]], y_first[1][:])
        nc.vector.tensor_copy(ds[0][:, halves[1]], y_ps[0][:, halves[1]])
        nc.scalar.copy(ds[1][:, halves[1]], y_ps[1][:, halves[1]])
        for t in range(PACK):
            if t in (1, 2):
                nc.scalar.copy(ds[t + 1][:], y_ps[t + 1][:])
            nc.scalar.activation(pa[t], ds[t][:].indirect(n1_t[:]), COPY)
            if t == 0:
                nc.vector.tensor_copy(pb[t], ds[t][:].indirect(n2_t[:]))
            else:
                nc.scalar.activation(pb[t], ds[t][:].indirect(n2_t[:]), COPY)
            nc.vector.tensor_tensor(ra[t][:], pa[t], pb[t], ALU.max)
            if t == 2:
                w1s = sb.tile([P, N], U8, name="w1s", tag="pa2", align_bytes=64)
                nc.vector.tensor_copy(
                    w1s[:].rearrange("p (t m) -> p t m", t=PACK), w1s_raw[:].rearrange("p (m t) -> p t m", t=PACK)
                )
            if t == 3:
                z_vector(2, full)
            nc.vector.tensor_copy(ds[t][:].indirect(n1_t[:]), ra[t][:])

        z_scalar(0, full)
        z_scalar(1, full)

        tab_gather(0, 1)
        for t in range(1, PACK):
            tab_gather(t, 0)
            tab_gather(t, 1)

        z_b = sb.tile([P, H, 2], F32, name="z_b", align_bytes=64)
        z_q = sb.tile([P, H], U32, name="z_q", align_bytes=64)
        z_s = sb.tile([P, H], U8, name="z_s", align_bytes=64)
        for c in halves:
            z_vector(3, c)
        for c in halves:
            nc.vector.tensor_copy(z_b[:, c, :], zw_all[:].rearrange("p (u c) -> p c u", u=2)[:, c, :])
        for c in halves:
            nc.vector.quantize_mx(
                out=z_q[:, c].bitcast(FP8X4), scales=z_s[:, c],
                in_=z_b[:, c, :].rearrange("p c u -> p (c u)").bitcast(BF16),
            )

        h_ps = [
            [psum.tile([P, HALF], F32, name="h_ps%d_%d" % (t, u), tag=("y_ps%d", "h_ps%d")[u] % t) for u in range(2)]
            for t in range(PACK)
        ]
        for pair in range(2):
            for u, c in enumerate(halves):
                for t in (2 * pair, 2 * pair + 1):
                    nc.tensor.matmul_mx(
                        out=h_ps[t][u][:], lhsT=w1w[:, 2 * P * t : 2 * P * (t + 1)].bitcast(FP4X4),
                        lhsT_scale=w1s[:, P * t : P * (t + 1)],
                        rhs=z_q[:, c].bitcast(FP8X4), rhs_scale=z_s[:, c], start=True, stop=True,
                    )

        hs = [sb.tile([P, H], F32, name="hs%d" % t, align_bytes=64) for t in range(PACK)]
        hm = sb.tile([P, PACK, H], F32, name="hm", align_bytes=64)
        hg = sb.tile([P, PACK, H], F32, name="hg", align_bytes=64)
        res = sb.tile([P, PACK, H], F32, name="res", align_bytes=64)

        chunks = [slice(P * k, P * (k + 1)) for k in range(4)]

        def h_copy(t, u):
            copy = nc.scalar.copy if t == 0 else nc.vector.tensor_copy
            copy(hs[t][:, halves[u]], h_ps[t][u][:])

        def h_mult(t, u):
            c = halves[u]
            if t < 2:
                nc.gpsimd.tensor_tensor(hm[:, t, c], hs[t][:, c], tabg[t][:, c], ALU.mult)
            else:
                nc.vector.tensor_tensor(hm[:, t, c], h_ps[t][u][:], tabg[t][:, c], ALU.mult)

        def h_gather(t, c):
            picked = hs[t][:].indirect(n4_t[:, c.start // 16 : c.stop // 16])
            if (t, c) == (2, chunks[0]):
                nc.vector.tensor_copy(hg[:, t, c], picked)
            else:
                nc.scalar.activation(hg[:, t, c], picked, COPY)

        o_b = sb.tile([P, H, PACK], BF16, name="o_b", align_bytes=64)
        o_q = sb.tile([P, H], U32, name="o_q", align_bytes=64)
        o_s = sb.tile([P, H], U8, name="o_s", align_bytes=64)
        out_v = out_0.rearrange("(p t) c -> p t c", t=PACK)
        words_v = out_1[0].rearrange("p n t -> p (n t)").bitcast(I32)

        def h_add(rows, c):
            nc.vector.scalar_tensor_tensor(res[:, rows, c], hg[:, rows, c], -0.5, hm[:, rows, c], ALU.mult, ALU.add)

        def o_round(c, copy):
            copy(o_b[:, c, :].rearrange("p (c i) j -> p c j i", i=4), res[:, :, c].rearrange("p j (c i) -> p c j i", i=4))

        def o_quantise(c):
            nc.vector.quantize_mx(
                out=o_q[:, c].bitcast(FP8X4), scales=o_s[:, c], in_=o_b[:, c, :].rearrange("p c j -> p (c j)")
            )

        for pair in range(2):
            for u in range(2):
                for t in (2 * pair, 2 * pair + 1):
                    h_copy(t, u)
        for u in range(2):
            for t in range(PACK):
                h_mult(t, u)
        early, late = slice(0, 2), slice(2, PACK)
        for c in halves:
            for t in range(2):
                h_gather(t, c)
            h_add(early, c)
        nc.sync.dma_start(out_v[:, early, :], res[:, early, :])
        for step in range(6):
            if step < 4:
                for t in range(2, PACK):
                    h_gather(t, chunks[step])
                h_add(late, chunks[step])
                if step >= 2:
                    c = slice(0, 384) if step == 2 else chunks[step]
                    nc.sync.dma_start(out_v[:, late, c], res[:, late, c])
            if step == 4:
                o_quantise(chunks[1])
            if 1 <= step < 5:
                o_round(chunks[step - 1], nc.scalar.copy if step == 3 else nc.vector.tensor_copy)
            if step in (2, 4, 5):
                o_quantise(chunks[step - 2])
            if step >= 4:
                c = slice(0, 384) if step == 4 else chunks[3]
                nc.sync.dma_start(words_v[:, c], o_q[:, c].bitcast(I32))
        for q in range(4):
            eng = nc.scalar if q % 2 == 0 else nc.sync
            eng.dma_start(out_2[0, 4 * q : 4 * q + 4, :].bitcast(I32), o_s[32 * q : 32 * q + 4, :].bitcast(I32))
